import numpy as np
import ml_dtypes

BF16 = ml_dtypes.bfloat16


def bf(x):
    return np.asarray(x, np.float32).astype(BF16)


def f32(x):
    return np.asarray(x, np.float32)


def f64(x):
    return np.asarray(x).astype(np.float64)


def striped(idx):
    return np.tile(idx.reshape(-1, 16).T, (8, 1))


S, K, M, N = 1024, 512, 256, 1024


def setup_inputs():
    return {"table": bf(np.random.standard_normal((K, S))), "w": bf(np.random.standard_normal((K, M)) / np.sqrt(K)), "s": f32(0.5 + np.random.random_sample((M, 1))), "b": f32(0.5 * np.random.standard_normal((M, 1))), "offs": striped(np.random.permutation(S))}


def reference(table, w, s, b, offs):
    idx = offs[:16].T.reshape(-1)
    x = f64(table)[:, idx]
    y = f64(w).T @ x
    return y * f64(s) + f64(b)

@@ -1,0 +1,59 @@
+import concourse.mybir as mybir
+
+BF16, F32, U16 = mybir.dt.bfloat16, mybir.dt.float32, mybir.dt.uint16
+MULT, ADD = mybir.AluOpType.mult, mybir.AluOpType.add
+
+P = 128
+K, S, M, N = 512, 1024, 256, 1024
+PIECE = 512
+K_BLOCKS = K // P
+M_BLOCKS = M // P
+PIECES = N // PIECE
+PIECE_COLS = PIECE // 16
+
+PSUM_SLOTS = 3
+
+FLOPS = 2 * K * M * N
+
+
+def tile_gather_matmul_kernel(tc, table, w, s, b, offs, out):
+    nc = tc.nc
+    with (
+        tc.tile_pool(name="held", bufs=1) as held,
+        tc.psum_pool(name="psum", bufs=PSUM_SLOTS) as psum,
+    ):
+        offsets = held.tile([P, N // 16], U16, name="offsets")
+        table_blocks = [held.tile([P, S], BF16, name="table_block%d" % kb) for kb in range(K_BLOCKS)]
+        w_blocks = [held.tile([P, M], BF16, name="w_block%d" % kb) for kb in range(K_BLOCKS)]
+        gain = held.tile([P, M_BLOCKS], F32, name="gain")
+        shift = held.tile([P, M_BLOCKS], F32, name="shift")
+
+        nc.sync.dma_start(offsets[:], offs)
+        nc.scalar.dma_start(table_blocks[0][:], table[0:P, :])
+        nc.sync.dma_start(w_blocks[0][:], w[0:P, :])
+        for kb in range(1, K_BLOCKS):
+            nc.scalar.dma_start(w_blocks[kb][:], w[kb * P : (kb + 1) * P, :])
+            nc.scalar.dma_start(table_blocks[kb][:], table[kb * P : (kb + 1) * P, :])
+        nc.scalar.dma_start(gain[:], s.rearrange("(a p) o -> p (a o)", p=P))
+        nc.scalar.dma_start(shift[:], b.rearrange("(a p) o -> p (a o)", p=P))
+
+        for mb in range(M_BLOCKS):
+            for piece in range(PIECES):
+                bank = psum.tile([P, PIECE], F32, name="bank")
+                piece_offsets = offsets[:, piece * PIECE_COLS : (piece + 1) * PIECE_COLS]
+                for kb in range(K_BLOCKS):
+                    nc.tensor.matmul(
+                        bank[:],
+                        w_blocks[kb][:, mb * P : (mb + 1) * P],
+                        table_blocks[kb][:].indirect(piece_offsets),
+                        start=(kb == 0),
+                        stop=(kb == K_BLOCKS - 1),
+                    )
+                result = held.tile([P, PIECE], F32, name="result%d_%d" % (mb, piece))
+                nc.vector.tensor_scalar(
+                    result[:], bank[:], gain[:, mb : mb + 1], shift[:, mb : mb + 1], MULT, ADD
+                )
+                store_queue = nc.sync if piece % 2 == 0 else nc.scalar
+                store_queue.dma_start(
+                    out[mb * P : (mb + 1) * P, piece * PIECE : (piece + 1) * PIECE], result[:]
+                )

@@ -11,8 +11,6 @@ M_BLOCKS = M // P
 PIECES = N // PIECE
 PIECE_COLS = PIECE // 16
 
-PSUM_SLOTS = 3
-
 FLOPS = 2 * K * M * N
 
 
@@ -20,22 +18,25 @@ def tile_gather_matmul_kernel(tc, table, w, s, b, offs, out):
     nc = tc.nc
     with (
         tc.tile_pool(name="held", bufs=1) as held,
-        tc.psum_pool(name="psum", bufs=PSUM_SLOTS) as psum,
+        tc.psum_pool(name="psum", bufs=M_BLOCKS * PIECES) as psum,
     ):
         offsets = held.tile([P, N // 16], U16, name="offsets")
         table_blocks = [held.tile([P, S], BF16, name="table_block%d" % kb) for kb in range(K_BLOCKS)]
-        w_blocks = [held.tile([P, M], BF16, name="w_block%d" % kb) for kb in range(K_BLOCKS)]
+        w_first = [held.tile([P, P], BF16, name="w_first%d" % kb) for kb in range(K_BLOCKS)]
+        w_second = held.tile([P, K_BLOCKS, P], BF16, name="w_second")
         gain = held.tile([P, M_BLOCKS], F32, name="gain")
         shift = held.tile([P, M_BLOCKS], F32, name="shift")
 
         nc.sync.dma_start(offsets[:], offs)
         nc.scalar.dma_start(table_blocks[0][:], table[0:P, :])
-        nc.sync.dma_start(w_blocks[0][:], w[0:P, :])
+        nc.sync.dma_start(w_first[0][:], w[0:P, 0:P])
         for kb in range(1, K_BLOCKS):
-            nc.scalar.dma_start(w_blocks[kb][:], w[kb * P : (kb + 1) * P, :])
+            nc.scalar.dma_start(w_first[kb][:], w[kb * P : (kb + 1) * P, 0:P])
             nc.scalar.dma_start(table_blocks[kb][:], table[kb * P : (kb + 1) * P, :])
+        nc.scalar.dma_start(w_second[:], w[:, P : 2 * P].rearrange("(kb p) m -> p kb m", p=P))
         nc.scalar.dma_start(gain[:], s.rearrange("(a p) o -> p (a o)", p=P))
         nc.scalar.dma_start(shift[:], b.rearrange("(a p) o -> p (a o)", p=P))
+        weights = [[w_first[kb][:] for kb in range(K_BLOCKS)], [w_second[:, kb, :] for kb in range(K_BLOCKS)]]
 
         for mb in range(M_BLOCKS):
             for piece in range(PIECES):
@@ -44,7 +45,7 @@ def tile_gather_matmul_kernel(tc, table, w, s, b, offs, out):
                 for kb in range(K_BLOCKS):
                     nc.tensor.matmul(
                         bank[:],
-                        w_blocks[kb][:, mb * P : (mb + 1) * P],
+                        weights[mb][kb],
                         table_blocks[kb][:].indirect(piece_offsets),
                         start=(kb == 0),
                         stop=(kb == K_BLOCKS - 1),

@@ -31,8 +31,8 @@ def tile_gather_matmul_kernel(tc, table, w, s, b, offs, out):
         nc.scalar.dma_start(table_blocks[0][:], table[0:P, :])
         nc.sync.dma_start(w_first[0][:], w[0:P, 0:P])
         for kb in range(1, K_BLOCKS):
-            nc.scalar.dma_start(w_first[kb][:], w[kb * P : (kb + 1) * P, 0:P])
             nc.scalar.dma_start(table_blocks[kb][:], table[kb * P : (kb + 1) * P, :])
+            nc.scalar.dma_start(w_first[kb][:], w[kb * P : (kb + 1) * P, 0:P])
         nc.scalar.dma_start(w_second[:], w[:, P : 2 * P].rearrange("(kb p) m -> p kb m", p=P))
         nc.scalar.dma_start(gain[:], s.rearrange("(a p) o -> p (a o)", p=P))
         nc.scalar.dma_start(shift[:], b.rearrange("(a p) o -> p (a o)", p=P))

@@ -28,14 +28,14 @@ def tile_gather_matmul_kernel(tc, table, w, s, b, offs, out):
         shift = held.tile([P, M_BLOCKS], F32, name="shift")
 
         nc.sync.dma_start(offsets[:], offs)
-        nc.scalar.dma_start(table_blocks[0][:], table[0:P, :])
         nc.sync.dma_start(w_first[0][:], w[0:P, 0:P])
+        nc.sync.dma_start(table_blocks[0][:], table[0:P, :])
         for kb in range(1, K_BLOCKS):
-            nc.scalar.dma_start(table_blocks[kb][:], table[kb * P : (kb + 1) * P, :])
-            nc.scalar.dma_start(w_first[kb][:], w[kb * P : (kb + 1) * P, 0:P])
-        nc.scalar.dma_start(w_second[:], w[:, P : 2 * P].rearrange("(kb p) m -> p kb m", p=P))
-        nc.scalar.dma_start(gain[:], s.rearrange("(a p) o -> p (a o)", p=P))
-        nc.scalar.dma_start(shift[:], b.rearrange("(a p) o -> p (a o)", p=P))
+            nc.sync.dma_start(table_blocks[kb][:], table[kb * P : (kb + 1) * P, :])
+            nc.sync.dma_start(w_first[kb][:], w[kb * P : (kb + 1) * P, 0:P])
+        nc.sync.dma_start(w_second[:], w[:, P : 2 * P].rearrange("(kb p) m -> p kb m", p=P))
+        nc.sync.dma_start(gain[:], s.rearrange("(a p) o -> p (a o)", p=P))
+        nc.sync.dma_start(shift[:], b.rearrange("(a p) o -> p (a o)", p=P))
         weights = [[w_first[kb][:] for kb in range(K_BLOCKS)], [w_second[:, kb, :] for kb in range(K_BLOCKS)]]
 
         for mb in range(M_BLOCKS):

@@ -27,9 +27,9 @@ def tile_gather_matmul_kernel(tc, table, w, s, b, offs, out):
         gain = held.tile([P, M_BLOCKS], F32, name="gain")
         shift = held.tile([P, M_BLOCKS], F32, name="shift")
 
+        nc.sync.dma_start(table_blocks[0][:], table[0:P, :])
         nc.sync.dma_start(offsets[:], offs)
         nc.sync.dma_start(w_first[0][:], w[0:P, 0:P])
-        nc.sync.dma_start(table_blocks[0][:], table[0:P, :])
         for kb in range(1, K_BLOCKS):
             nc.sync.dma_start(table_blocks[kb][:], table[kb * P : (kb + 1) * P, :])
             nc.sync.dma_start(w_first[kb][:], w[kb * P : (kb + 1) * P, 0:P])
@@ -54,7 +54,6 @@ def tile_gather_matmul_kernel(tc, table, w, s, b, offs, out):
                 nc.vector.tensor_scalar(
                     result[:], bank[:], gain[:, mb : mb + 1], shift[:, mb : mb + 1], MULT, ADD
                 )
-                store_queue = nc.sync if piece % 2 == 0 else nc.scalar
-                store_queue.dma_start(
+                nc.sync.dma_start(
                     out[mb * P : (mb + 1) * P, piece * PIECE : (piece + 1) * PIECE], result[:]
                 )

@@ -50,10 +50,19 @@ def tile_gather_matmul_kernel(tc, table, w, s, b, offs, out):
                         start=(kb == 0),
                         stop=(kb == K_BLOCKS - 1),
                     )
+                last_tile = mb == M_BLOCKS - 1 and piece == PIECES - 1
+                part = PIECE // 2 if last_tile else PIECE
                 result = held.tile([P, PIECE], F32, name="result%d_%d" % (mb, piece))
-                nc.vector.tensor_scalar(
-                    result[:], bank[:], gain[:, mb : mb + 1], shift[:, mb : mb + 1], MULT, ADD
-                )
-                nc.sync.dma_start(
-                    out[mb * P : (mb + 1) * P, piece * PIECE : (piece + 1) * PIECE], result[:]
-                )
+                for first in range(0, PIECE, part):
+                    nc.vector.tensor_scalar(
+                        result[:, first : first + part],
+                        bank[:, first : first + part],
+                        gain[:, mb : mb + 1],
+                        shift[:, mb : mb + 1],
+                        MULT,
+                        ADD,
+                    )
+                    nc.sync.dma_start(
+                        out[mb * P : (mb + 1) * P, piece * PIECE + first : piece * PIECE + first + part],
+                        result[:, first : first + part],
+                    )

@@ -22,21 +22,27 @@ def tile_gather_matmul_kernel(tc, table, w, s, b, offs, out):
     ):
         offsets = held.tile([P, N // 16], U16, name="offsets")
         table_blocks = [held.tile([P, S], BF16, name="table_block%d" % kb) for kb in range(K_BLOCKS)]
-        w_first = [held.tile([P, P], BF16, name="w_first%d" % kb) for kb in range(K_BLOCKS)]
+        w_first_early = [held.tile([P, P], BF16, name="w_first%d" % kb) for kb in range(2)]
+        w_first_late = held.tile([P, K_BLOCKS - 2, P], BF16, name="w_first_late")
         w_second = held.tile([P, K_BLOCKS, P], BF16, name="w_second")
         gain = held.tile([P, M_BLOCKS], F32, name="gain")
         shift = held.tile([P, M_BLOCKS], F32, name="shift")
 
         nc.sync.dma_start(table_blocks[0][:], table[0:P, :])
         nc.sync.dma_start(offsets[:], offs)
-        nc.sync.dma_start(w_first[0][:], w[0:P, 0:P])
-        for kb in range(1, K_BLOCKS):
-            nc.sync.dma_start(table_blocks[kb][:], table[kb * P : (kb + 1) * P, :])
-            nc.sync.dma_start(w_first[kb][:], w[kb * P : (kb + 1) * P, 0:P])
+        nc.sync.dma_start(w_first_early[0][:], w[0:P, 0:P])
+        nc.sync.dma_start(table_blocks[1][:], table[P : 2 * P, :])
+        nc.sync.dma_start(w_first_early[1][:], w[P : 2 * P, 0:P])
+        nc.sync.dma_start(table_blocks[2][:], table[2 * P : 3 * P, :])
+        nc.sync.dma_start(w_first_late[:], w[2 * P : K, 0:P].rearrange("(kb p) m -> p kb m", p=P))
+        nc.sync.dma_start(table_blocks[3][:], table[3 * P : K, :])
         nc.sync.dma_start(w_second[:], w[:, P : 2 * P].rearrange("(kb p) m -> p kb m", p=P))
         nc.sync.dma_start(gain[:], s.rearrange("(a p) o -> p (a o)", p=P))
         nc.sync.dma_start(shift[:], b.rearrange("(a p) o -> p (a o)", p=P))
-        weights = [[w_first[kb][:] for kb in range(K_BLOCKS)], [w_second[:, kb, :] for kb in range(K_BLOCKS)]]
+        weights = [
+            [w_first_early[0][:], w_first_early[1][:], w_first_late[:, 0, :], w_first_late[:, 1, :]],
+            [w_second[:, kb, :] for kb in range(K_BLOCKS)],
+        ]
 
         for mb in range(M_BLOCKS):
             for piece in range(PIECES):

import concourse.mybir as mybir

BF16, F32, U16 = mybir.dt.bfloat16, mybir.dt.float32, mybir.dt.uint16
MULT, ADD = mybir.AluOpType.mult, mybir.AluOpType.add

P = 128
K, S, M, N = 512, 1024, 256, 1024
PIECE = 512
K_BLOCKS = K // P
M_BLOCKS = M // P
PIECES = N // PIECE
PIECE_COLS = PIECE // 16

FLOPS = 2 * K * M * N


def tile_gather_matmul_kernel(tc, table, w, s, b, offs, out):
    nc = tc.nc
    with (
        tc.tile_pool(name="held", bufs=1) as held,
        tc.psum_pool(name="psum", bufs=M_BLOCKS * PIECES) as psum,
    ):
        offsets = held.tile([P, N // 16], U16, name="offsets")
        table_blocks = [held.tile([P, S], BF16, name="table_block%d" % kb) for kb in range(K_BLOCKS)]
        w_first_early = [held.tile([P, P], BF16, name="w_first%d" % kb) for kb in range(2)]
        w_first_late = held.tile([P, K_BLOCKS - 2, P], BF16, name="w_first_late")
        w_second = held.tile([P, K_BLOCKS, P], BF16, name="w_second")
        gain = held.tile([P, M_BLOCKS], F32, name="gain")
        shift = held.tile([P, M_BLOCKS], F32, name="shift")

        nc.sync.dma_start(table_blocks[0][:], table[0:P, :])
        nc.sync.dma_start(offsets[:], offs)
        nc.sync.dma_start(w_first_early[0][:], w[0:P, 0:P])
        nc.sync.dma_start(table_blocks[1][:], table[P : 2 * P, :])
        nc.sync.dma_start(w_first_early[1][:], w[P : 2 * P, 0:P])
        nc.sync.dma_start(table_blocks[2][:], table[2 * P : 3 * P, :])
        nc.sync.dma_start(w_first_late[:], w[2 * P : K, 0:P].rearrange("(kb p) m -> p kb m", p=P))
        nc.sync.dma_start(table_blocks[3][:], table[3 * P : K, :])
        nc.sync.dma_start(w_second[:], w[:, P : 2 * P].rearrange("(kb p) m -> p kb m", p=P))
        nc.sync.dma_start(gain[:], s.rearrange("(a p) o -> p (a o)", p=P))
        nc.sync.dma_start(shift[:], b.rearrange("(a p) o -> p (a o)", p=P))
        weights = [
            [w_first_early[0][:], w_first_early[1][:], w_first_late[:, 0, :], w_first_late[:, 1, :]],
            [w_second[:, kb, :] for kb in range(K_BLOCKS)],
        ]

        for mb in range(M_BLOCKS):
            for piece in range(PIECES):
                bank = psum.tile([P, PIECE], F32, name="bank")
                piece_offsets = offsets[:, piece * PIECE_COLS : (piece + 1) * PIECE_COLS]
                for kb in range(K_BLOCKS):
                    nc.tensor.matmul(
                        bank[:],
                        weights[mb][kb],
                        table_blocks[kb][:].indirect(piece_offsets),
                        start=(kb == 0),
                        stop=(kb == K_BLOCKS - 1),
                    )
                last_tile = mb == M_BLOCKS - 1 and piece == PIECES - 1
                part = PIECE // 2 if last_tile else PIECE
                result = held.tile([P, PIECE], F32, name="result%d_%d" % (mb, piece))
                for first in range(0, PIECE, part):
                    nc.vector.tensor_scalar(
                        result[:, first : first + part],
                        bank[:, first : first + part],
                        gain[:, mb : mb + 1],
                        shift[:, mb : mb + 1],
                        MULT,
                        ADD,
                    )
                    nc.sync.dma_start(
                        out[mb * P : (mb + 1) * P, piece * PIECE + first : piece * PIECE + first + part],
                        result[:, first : first + part],
                    )
